import numpy as np
import ml_dtypes


def mxq(x, axis, fmt="e4m3"):
    dtype, down = {"e4m3": (ml_dtypes.float8_e4m3fn, 7), "e5m2": (ml_dtypes.float8_e5m2, 14)}[fmt]
    v = np.moveaxis(np.asarray(x, np.float32).astype(ml_dtypes.bfloat16).astype(np.float64), axis, -1)
    blocks = v.reshape(v.shape[:-1] + (-1, 32))
    amax = np.abs(blocks).max(-1, keepdims=True)
    byte = np.maximum(np.where(amax > 0, np.frexp(amax)[1] - 1 + 127, 0) - down, 1)
    scale = np.exp2(byte - 127.0)
    codes = (blocks / scale).astype(np.float32).astype(dtype).astype(np.float64)
    return np.moveaxis((codes * scale).reshape(v.shape), -1, axis)


WIDE = False


def mx_kscale(k):
    if not WIDE:
        return np.ones(k)
    levels = np.array([10, -10, 5, -5, 0])
    if k % 512:
        return np.exp2(np.random.permutation(np.resize(levels, k // 32))).repeat(32)
    a = np.empty((k // 512, 16))
    for p in range(k // 512):
        a[p, :8] = np.random.permutation(np.resize(levels, 8))
        for g in range(8):
            far = levels[np.abs(levels - a[p, g]) >= 10]
            a[p, g + 8] = far[np.random.randint(len(far))]
    return np.exp2(a.ravel()).repeat(32)


def f64(x):
    return np.asarray(x).astype(np.float64)


def striped(idx):
    return np.tile(np.asarray(idx).reshape(-1, 16).T, (8, 1)).astype(np.uint16)


def unstriped(offs):
    return offs[:16].T.reshape(-1).astype(np.int64)


E2M1 = np.array([0.0, 0.5, 1.0, 1.5, 2.0, 3.0, 4.0, 6.0, -0.0, -0.5, -1.0, -1.5, -2.0, -3.0, -4.0, -6.0])


def pack_weight(w, fmt):
    k, n = w.shape
    w = f64(np.asarray(w, np.float32).astype(ml_dtypes.bfloat16)).reshape(k // 32, 32, n)
    amax = np.abs(w).max(1)
    if fmt == "e4m3":
        byte = np.frexp(amax)[1] - 1 + 127 - 7
    else:
        mant, ex = np.frexp(amax / 6.0)
        byte = np.where(mant > 0.5, ex, ex - 1) + 127
    byte = np.clip(np.where(amax > 0, byte, 1), 1, 254)
    scaled = (w * np.exp2(127.0 - byte)[:, None, :]).reshape(k, n).astype(np.float32)
    by_word = np.ascontiguousarray(scaled.reshape(k // 512, 128, 4, n).transpose(0, 1, 3, 2))
    if fmt == "e4m3":
        words = by_word.astype(ml_dtypes.float8_e4m3fn).view(np.uint8)
    else:
        c = by_word.astype(ml_dtypes.float4_e2m1fn).view(np.uint8) & 0xF
        words = (c[..., 0::2] | (c[..., 1::2] << 4)).reshape(k // 512, 128, 2 * n)
    return np.ascontiguousarray(words), np.ascontiguousarray(byte.astype(np.uint8).reshape(k // 512, 16, n))


def unpack_weight(words, scales, fmt):
    g, _, n = scales.shape
    words = np.ascontiguousarray(words).reshape(g, 128, n, -1)
    if fmt == "e4m3":
        vals = words.view(ml_dtypes.float8_e4m3fn).astype(np.float64)
    else:
        nib = np.empty((g, 128, n, 4), np.uint8)
        nib[..., 0::2] = words & 0xF
        nib[..., 1::2] = words >> 4
        vals = E2M1[nib]
    vals = vals * np.repeat(np.exp2(scales.astype(np.float64) - 127.0), 8, axis=1)[..., None]
    return vals.transpose(0, 1, 3, 2).reshape(g * 512, n)


D, E, T, I, Q = 512, 512, 2048, 512, 128


def setup_inputs():
    n = np.random.standard_normal
    idx = np.random.permutation(T)[:I]
    fd = mx_kscale(D)
    fe = mx_kscale(E)
    keysp = pack_weight(n((D, T)) / fd[:, None], "e4m3")
    valsp = pack_weight(n((E, T)) / fe[:, None], "e4m3")
    return {
        "query": (n((D, Q)) * 1.0 / np.sqrt(D) * fd[:, None]).astype(np.float32),
        "keys_words": keysp[0],
        "keys_scales": keysp[1],
        "floor": (np.random.uniform(0.05, 0.3, (Q, 1))).astype(np.float32),
        "reserve": (np.random.uniform(20.0, 100.0, (Q, 1))).astype(np.float32),
        "gout": (n((E, Q)) * 1 / np.sqrt(E) * fe[:, None]).astype(np.float32),
        "vals_words": valsp[0],
        "vals_scales": valsp[1],
        "dquery": (n((D, Q)) * 1.0 / np.sqrt(D) * fd[:, None]).astype(np.float32),
        "base": (0.5 * n((Q, T))).astype(np.float32),
        "offs": striped(idx),
    }


def reference(query, keys_words, keys_scales, floor, reserve, gout, vals_words, vals_scales, dquery, base, offs):
    idx = unstriped(offs)
    keysu = unpack_weight(keys_words, keys_scales, "e4m3")
    valsu = unpack_weight(vals_words, vals_scales, "e4m3")
    queryq = mxq(f64(query), 0, "e4m3")
    keysidxg = keysu[:, idx]
    a = queryq.T @ keysidxg
    dqueryq = mxq(f64(dquery), 0, "e4m3")
    ta = dqueryq.T @ keysidxg
    p = np.square(a) + f64(floor)
    z = np.sum(p, axis=1, keepdims=True) + f64(reserve)
    goutq = mxq(f64(gout), 0, "e4m3")
    valsidxg = valsu[:, idx]
    c0 = goutq.T @ valsidxg
    dz = np.sum(c0 * p / np.square(z) * (-1.0), axis=1, keepdims=True)
    dp = c0 / z + dz
    tp = ta * a * 2.0
    tz = np.sum(tp, axis=1, keepdims=True)
    tdz = np.sum((tp * c0 - tz * z * 2.0 * c0 * p / np.square(z)) / np.square(z) * (-1.0), axis=1, keepdims=True)
    tdp = tz * c0 / np.square(z) * (-1.0) + tdz
    tda = (tdp * a + ta * dp) * 2.0
    gs = tda * 512.0
    gf = np.zeros((Q, T))
    gf[:, idx] = gs
    y = f64(base) + gf
    return y

@@ -1,0 +1,163 @@
+from contextlib import ExitStack
+
+import concourse.mybir as mybir
+
+D, T, I, Q = 512, 2048, 512, 128
+FLOPS = 3 * 2 * D * Q * I
+
+F32 = mybir.dt.float32
+BF16 = mybir.dt.bfloat16
+I32 = mybir.dt.int32
+U32 = mybir.dt.uint32
+U16 = mybir.dt.uint16
+U8 = mybir.dt.uint8
+FP8X4 = mybir.dt.float8_e4m3fn_x4
+ALU = mybir.AluOpType
+ACT = mybir.ActivationFunctionType
+
+P = 128
+PACK = 4
+VALS_ROW0 = 4
+STORE_WIDTHS = (256, 512, 512, 512, 256)
+
+
+def tile_attend_hvsquareshares_s_kernel(
+    tc, query, keys_words, keys_scales, floor, reserve, gout, vals_words, vals_scales, dquery, base, offs, out
+):
+    nc = tc.nc
+    with ExitStack() as ctx:
+        keep = ctx.enter_context(tc.tile_pool(name="keep", bufs=1))
+        psum = ctx.enter_context(tc.psum_pool(name="psum", bufs=1))
+
+        def sb(name, width, dtype):
+            return keep.tile([P, width], dtype, name=name, align_bytes=64)
+
+        offsets = keep.tile([P, I // 16], U16, name="offsets")
+        nc.sync.dma_start(offsets[:], offs)
+
+        def load_scales(name, scales, row0, queue):
+            plane = sb(name, T, U8)
+            nc.vector.memset(plane[:].bitcast(I32), 0)
+            for quad in range(4):
+                queue.dma_start(
+                    plane[32 * quad + row0 : 32 * quad + row0 + 4, :].bitcast(I32),
+                    scales[0, 4 * quad : 4 * quad + 4, :].bitcast(I32),
+                )
+            return plane
+
+        def load_words(name, words):
+            pool = sb(name, T, I32)
+            nc.sync.dma_start(pool[:], words[0].rearrange("p n t -> p (n t)").bitcast(I32))
+            return pool
+
+        def load_rows(name, rows):
+            raw = keep.tile([P, PACK, Q], F32, name=name)
+            nc.sync.dma_start(raw[:], rows.rearrange("(p j) q -> p j q", j=PACK))
+            return raw
+
+        def gather(name, pool, dtype):
+            picked = sb(name, I, dtype)
+            nc.vector.tensor_copy(picked[:], pool.indirect(offsets[:]))
+            return picked
+
+        def quantise(name, raw):
+            woven = keep.tile([P, Q, PACK], BF16, name=name + "_woven", align_bytes=64)
+            nc.scalar.copy(woven[:], raw[:].rearrange("p j q -> p q j"))
+            codes = sb(name + "_codes", Q, U32)
+            plane = sb(name + "_plane", Q, U8)
+            nc.vector.quantize_mx(
+                out=codes[:].bitcast(FP8X4), scales=plane[:], in_=woven[:].rearrange("p q j -> p (q j)")
+            )
+            return codes, plane
+
+        def scores(name, rows, words, plane):
+            bank = psum.tile([P, I], F32, name=name)
+            nc.tensor.matmul_mx(
+                out=bank[:], lhsT=rows[0][:].bitcast(FP8X4), lhsT_scale=rows[1][:],
+                rhs=words[:].bitcast(FP8X4), rhs_scale=plane, start=True, stop=True,
+            )
+            return bank
+
+        floor_sb = sb("floor_sb", 1, F32)
+        reserve_sb = sb("reserve_sb", 1, F32)
+        nc.gpsimd.dma_start(floor_sb[:], floor)
+        nc.gpsimd.dma_start(reserve_sb[:], reserve)
+
+        key_scale_pool = load_scales("key_scale_pool", keys_scales, 0, nc.scalar)
+        key_pool = load_words("key_pool", keys_words)
+        query_raw = load_rows("query_raw", query)
+        dquery_raw = load_rows("dquery_raw", dquery)
+        val_scale_pool = load_scales("val_scale_pool", vals_scales, VALS_ROW0, nc.sync)
+        val_pool = load_words("val_pool", vals_words)
+        gout_raw = load_rows("gout_raw", gout)
+        base_sb = sb("base_sb", T, F32)
+        nc.sync.dma_start(base_sb[:], base)
+        placed = sb("placed", T, F32)
+        nc.vector.memset(placed[:], 0.0)
+
+        key_plane = gather("key_plane", key_scale_pool[:], U8)
+        keys = gather("keys", key_pool[:].bitcast(U32), U32)
+        query_mx = quantise("query", query_raw)
+        dquery_mx = quantise("dquery", dquery_raw)
+        a = scores("a", query_mx, keys, key_plane[:])
+        ta = scores("ta", dquery_mx, keys, key_plane[:])
+        val_plane = gather("val_plane", val_scale_pool[:], U8)
+
+        floor_k = sb("floor_k", 1, F32)
+        nc.scalar.activation(floor_k[:], floor_sb[:], ACT.Identity, scale=1.0 / 1024)
+        reserve_k = sb("reserve_k", 1, F32)
+        nc.scalar.activation(reserve_k[:], reserve_sb[:], ACT.Identity, scale=-1.0 / 1024)
+        fixed = sb("fixed", 1, F32)
+        nc.scalar.activation(fixed[:], floor_sb[:], ACT.Identity, scale=-float(I) / 1024, bias=reserve_k[:])
+
+        a_sb = sb("a_sb", I, F32)
+        nc.scalar.copy(a_sb[:], a[:])
+        sq = sb("sq", I, F32)
+        sq_sum = sb("sq_sum", 1, F32)
+        nc.scalar.activation(sq[:], a[:], ACT.Square, scale=1.0 / 32, accum_out=sq_sum[:])
+        neg_z = sb("neg_z", 1, F32)
+        nc.scalar.activation(neg_z[:], sq_sum[:], ACT.Identity, scale=-1.0, bias=fixed[:])
+
+        at = sb("at", I, F32)
+        at_sum = sb("at_sum", 1, F32)
+        nc.vector.scalar_tensor_tensor(at[:], ta[:], -1.0 / 512, a_sb[:], ALU.mult, ALU.mult, accum_out=at_sum[:])
+        neg_alpha = sb("neg_alpha", 1, F32)
+        nc.vector.reciprocal(neg_alpha[:], neg_z[:])
+        alpha2 = sb("alpha2", 1, F32)
+        nc.scalar.activation(alpha2[:], neg_alpha[:], ACT.Square)
+        beta = sb("beta", 1, F32)
+        nc.scalar.activation(beta[:], at_sum[:], ACT.Identity, scale=alpha2[:])
+        neg_x = sb("neg_x", I, F32)
+        nc.scalar.activation(neg_x[:], ta[:], ACT.Identity, scale=neg_alpha[:])
+
+        vals = gather("vals", val_pool[:].bitcast(U32), U32)
+        gout_mx = quantise("gout", gout_raw)
+        c0 = scores("c0", gout_mx, vals, val_plane[VALS_ROW0:P, :])
+
+        w = sb("w", I, F32)
+        nc.vector.scalar_tensor_tensor(w[:], a_sb[:], beta[:], neg_x[:], ALU.mult, ALU.subtract)
+
+        cp = sb("cp", I, F32)
+        cp_sum = sb("cp_sum", 1, F32)
+        nc.vector.scalar_tensor_tensor(cp[:], sq[:], floor_k[:], c0[:], ALU.add, ALU.mult, accum_out=cp_sum[:])
+        cat = sb("cat", I, F32)
+        cat_sum = sb("cat_sum", 1, F32)
+        nc.vector.scalar_tensor_tensor(cat[:], at[:], alpha2[:], c0[:], ALU.mult, ALU.mult, accum_out=cat_sum[:])
+        eps = sb("eps", 1, F32)
+        nc.scalar.activation(eps[:], cp_sum[:], ACT.Identity, scale=neg_alpha[:])
+        gamma = sb("gamma", 1, F32)
+        nc.scalar.activation(gamma[:], eps[:], ACT.Identity, scale=beta[:], bias=cat_sum[:])
+        term_w = sb("term_w", I, F32)
+        nc.vector.scalar_tensor_tensor(term_w[:], c0[:], eps[:], w[:], ALU.add, ALU.mult)
+        term_a = sb("term_a", I, F32)
+        nc.scalar.activation(term_a[:], a[:], ACT.Identity, scale=gamma[:])
+
+        nc.vector.tensor_tensor(placed[:].indirect(offsets[:]), term_w[:], term_a[:], ALU.add)
+
+        start = 0
+        for n, width in enumerate(STORE_WIDTHS):
+            cols = slice(start, start + width)
+            piece = sb(f"piece{n}", width, F32)
+            nc.vector.tensor_tensor(piece[:], placed[:, cols], base_sb[:, cols], ALU.add)
+            nc.sync.dma_start(out[:, cols], piece[:])
+            start = start + width

@@ -18,6 +18,8 @@ ACT = mybir.ActivationFunctionType
 P = 128
 PACK = 4
 VALS_ROW0 = 4
+HALF = I // 2
+KEY_SPLIT = 3 * T // 4
 STORE_WIDTHS = (256, 512, 512, 512, 256)
 
 
@@ -29,78 +31,84 @@ def tile_attend_hvsquareshares_s_kernel(
         keep = ctx.enter_context(tc.tile_pool(name="keep", bufs=1))
         psum = ctx.enter_context(tc.psum_pool(name="psum", bufs=1))
 
-        def sb(name, width, dtype):
-            return keep.tile([P, width], dtype, name=name, align_bytes=64)
+        def sb(name, width, dtype, tag=None):
+            return keep.tile([P, width], dtype, name=name, tag=tag or name, align_bytes=64)
 
         offsets = keep.tile([P, I // 16], U16, name="offsets")
         nc.sync.dma_start(offsets[:], offs)
 
-        def load_scales(name, scales, row0, queue):
+        def load_scales(name, scales, row0, queues):
             plane = sb(name, T, U8)
             nc.vector.memset(plane[:].bitcast(I32), 0)
             for quad in range(4):
-                queue.dma_start(
+                queues[quad].dma_start(
                     plane[32 * quad + row0 : 32 * quad + row0 + 4, :].bitcast(I32),
                     scales[0, 4 * quad : 4 * quad + 4, :].bitcast(I32),
                 )
             return plane
 
-        def load_words(name, words):
-            pool = sb(name, T, I32)
-            nc.sync.dma_start(pool[:], words[0].rearrange("p n t -> p (n t)").bitcast(I32))
-            return pool
+        def load_words(pool, words, cols):
+            nc.sync.dma_start(pool[:, cols], words[0].rearrange("p n t -> p (n t)").bitcast(I32)[:, cols])
 
-        def load_rows(name, rows):
-            raw = keep.tile([P, PACK, Q], F32, name=name)
+        def load_rows(name, rows, tag):
+            raw = keep.tile([P, PACK, Q], F32, name=name, tag=tag, align_bytes=64)
             nc.sync.dma_start(raw[:], rows.rearrange("(p j) q -> p j q", j=PACK))
             return raw
 
-        def gather(name, pool, dtype):
-            picked = sb(name, I, dtype)
+        def gather(name, pool, dtype, tag=None):
+            picked = sb(name, I, dtype, tag)
             nc.vector.tensor_copy(picked[:], pool.indirect(offsets[:]))
             return picked
 
-        def quantise(name, raw):
+        def quantise(name, raw, tag=None):
             woven = keep.tile([P, Q, PACK], BF16, name=name + "_woven", align_bytes=64)
             nc.scalar.copy(woven[:], raw[:].rearrange("p j q -> p q j"))
-            codes = sb(name + "_codes", Q, U32)
+            codes = sb(name + "_codes", Q, U32, tag)
             plane = sb(name + "_plane", Q, U8)
             nc.vector.quantize_mx(
                 out=codes[:].bitcast(FP8X4), scales=plane[:], in_=woven[:].rearrange("p q j -> p (q j)")
             )
             return codes, plane
 
-        def scores(name, rows, words, plane):
-            bank = psum.tile([P, I], F32, name=name)
-            nc.tensor.matmul_mx(
-                out=bank[:], lhsT=rows[0][:].bitcast(FP8X4), lhsT_scale=rows[1][:],
-                rhs=words[:].bitcast(FP8X4), rhs_scale=plane, start=True, stop=True,
-            )
-            return bank
+        def gather_and_score(name, pool, plane, row0, products, tag=None):
+            picked = sb(name, I, U32, tag)
+            for lo in range(0, I, HALF):
+                cols = slice(lo, lo + HALF)
+                listed = offsets[:, lo // 16 : (lo + HALF) // 16]
+                nc.vector.tensor_copy(picked[:, cols], pool[:].bitcast(U32).indirect(listed))
+                for bank, (codes, code_plane) in products:
+                    nc.tensor.matmul_mx(
+                        out=bank[:, cols], lhsT=codes[:].bitcast(FP8X4), lhsT_scale=code_plane[:],
+                        rhs=picked[:, cols].bitcast(FP8X4), rhs_scale=plane[row0:P, cols], start=True, stop=True,
+                    )
 
         floor_sb = sb("floor_sb", 1, F32)
         reserve_sb = sb("reserve_sb", 1, F32)
-        nc.gpsimd.dma_start(floor_sb[:], floor)
-        nc.gpsimd.dma_start(reserve_sb[:], reserve)
+        nc.scalar.dma_start(floor_sb[:], floor)
+        nc.scalar.dma_start(reserve_sb[:], reserve)
 
-        key_scale_pool = load_scales("key_scale_pool", keys_scales, 0, nc.scalar)
-        key_pool = load_words("key_pool", keys_words)
-        query_raw = load_rows("query_raw", query)
-        dquery_raw = load_rows("dquery_raw", dquery)
-        val_scale_pool = load_scales("val_scale_pool", vals_scales, VALS_ROW0, nc.sync)
-        val_pool = load_words("val_pool", vals_words)
-        gout_raw = load_rows("gout_raw", gout)
+        key_pool = sb("key_pool", T, I32)
+        load_words(key_pool, keys_words, slice(0, KEY_SPLIT))
+        key_scale_pool = load_scales("key_scale_pool", keys_scales, 0, [nc.sync] * 4)
+        query_raw = load_rows("query_raw", query, "query_raw")
+        dquery_raw = load_rows("dquery_raw", dquery, "dquery_raw")
+        load_words(key_pool, keys_words, slice(KEY_SPLIT, T))
+        gout_raw = load_rows("gout_raw", gout, "gout_raw")
+        val_scale_pool = load_scales("val_scale_pool", vals_scales, VALS_ROW0, [nc.sync] * 4)
+        val_pool = sb("val_pool", T, I32)
+        load_words(val_pool, vals_words, slice(0, T))
         base_sb = sb("base_sb", T, F32)
         nc.sync.dma_start(base_sb[:], base)
         placed = sb("placed", T, F32)
         nc.vector.memset(placed[:], 0.0)
 
         key_plane = gather("key_plane", key_scale_pool[:], U8)
-        keys = gather("keys", key_pool[:].bitcast(U32), U32)
         query_mx = quantise("query", query_raw)
         dquery_mx = quantise("dquery", dquery_raw)
-        a = scores("a", query_mx, keys, key_plane[:])
-        ta = scores("ta", dquery_mx, keys, key_plane[:])
+        a = psum.tile([P, I], F32, name="a")
+        ta = psum.tile([P, I], F32, name="ta")
+        gather_and_score("keys", key_pool, key_plane, 0, ((a, query_mx), (ta, dquery_mx)))
+        gout_mx = quantise("gout", gout_raw)
         val_plane = gather("val_plane", val_scale_pool[:], U8)
 
         floor_k = sb("floor_k", 1, F32)
@@ -110,7 +118,7 @@ def tile_attend_hvsquareshares_s_kernel(
         fixed = sb("fixed", 1, F32)
         nc.scalar.activation(fixed[:], floor_sb[:], ACT.Identity, scale=-float(I) / 1024, bias=reserve_k[:])
 
-        a_sb = sb("a_sb", I, F32)
+        a_sb = sb("a_sb", I, F32, "gout_raw")
         nc.scalar.copy(a_sb[:], a[:])
         sq = sb("sq", I, F32)
         sq_sum = sb("sq_sum", 1, F32)
@@ -118,41 +126,43 @@ def tile_attend_hvsquareshares_s_kernel(
         neg_z = sb("neg_z", 1, F32)
         nc.scalar.activation(neg_z[:], sq_sum[:], ACT.Identity, scale=-1.0, bias=fixed[:])
 
-        at = sb("at", I, F32)
+        at_and_alpha = sb("at_and_alpha", I + 1, F32, "val_scale_pool")
+        at = at_and_alpha[:, 0:I]
+        neg_alpha = at_and_alpha[:, I : I + 1]
         at_sum = sb("at_sum", 1, F32)
-        nc.vector.scalar_tensor_tensor(at[:], ta[:], -1.0 / 512, a_sb[:], ALU.mult, ALU.mult, accum_out=at_sum[:])
-        neg_alpha = sb("neg_alpha", 1, F32)
-        nc.vector.reciprocal(neg_alpha[:], neg_z[:])
+        nc.vector.scalar_tensor_tensor(at, ta[:], -1.0 / 512, a_sb[:], ALU.mult, ALU.mult, accum_out=at_sum[:])
+        nc.vector.reciprocal(neg_alpha, neg_z[:])
         alpha2 = sb("alpha2", 1, F32)
-        nc.scalar.activation(alpha2[:], neg_alpha[:], ACT.Square)
+        nc.scalar.activation(alpha2[:], neg_alpha, ACT.Square)
         beta = sb("beta", 1, F32)
         nc.scalar.activation(beta[:], at_sum[:], ACT.Identity, scale=alpha2[:])
         neg_x = sb("neg_x", I, F32)
-        nc.scalar.activation(neg_x[:], ta[:], ACT.Identity, scale=neg_alpha[:])
+        nc.scalar.activation(neg_x[:], ta[:], ACT.Identity, scale=neg_alpha)
 
-        vals = gather("vals", val_pool[:].bitcast(U32), U32)
-        gout_mx = quantise("gout", gout_raw)
-        c0 = scores("c0", gout_mx, vals, val_plane[VALS_ROW0:P, :])
+        c0 = psum.tile([P, I], F32, name="c0")
+        gather_and_score("vals", val_pool, val_plane, VALS_ROW0, ((c0, gout_mx),), "gout_raw")
 
-        w = sb("w", I, F32)
-        nc.vector.scalar_tensor_tensor(w[:], a_sb[:], beta[:], neg_x[:], ALU.mult, ALU.subtract)
+        w = sb("w", I, F32, "val_pool")
+        nc.vector.scalar_tensor_tensor(w[:], a[:], beta[:], neg_x[:], ALU.mult, ALU.subtract)
 
         cp = sb("cp", I, F32)
         cp_sum = sb("cp_sum", 1, F32)
         nc.vector.scalar_tensor_tensor(cp[:], sq[:], floor_k[:], c0[:], ALU.add, ALU.mult, accum_out=cp_sum[:])
         cat = sb("cat", I, F32)
         cat_sum = sb("cat_sum", 1, F32)
-        nc.vector.scalar_tensor_tensor(cat[:], at[:], alpha2[:], c0[:], ALU.mult, ALU.mult, accum_out=cat_sum[:])
+        nc.vector.scalar_tensor_tensor(cat[:], at, alpha2[:], c0[:], ALU.mult, ALU.mult, accum_out=cat_sum[:])
         eps = sb("eps", 1, F32)
-        nc.scalar.activation(eps[:], cp_sum[:], ACT.Identity, scale=neg_alpha[:])
+        nc.scalar.activation(eps[:], cp_sum[:], ACT.Identity, scale=neg_alpha)
         gamma = sb("gamma", 1, F32)
         nc.scalar.activation(gamma[:], eps[:], ACT.Identity, scale=beta[:], bias=cat_sum[:])
         term_w = sb("term_w", I, F32)
         nc.vector.scalar_tensor_tensor(term_w[:], c0[:], eps[:], w[:], ALU.add, ALU.mult)
-        term_a = sb("term_a", I, F32)
-        nc.scalar.activation(term_a[:], a[:], ACT.Identity, scale=gamma[:])
-
-        nc.vector.tensor_tensor(placed[:].indirect(offsets[:]), term_w[:], term_a[:], ALU.add)
+        for n, (lo, hi) in enumerate(((0, I),)):
+            term_a = sb(f"term_a{n}", hi - lo, F32)
+            nc.scalar.activation(term_a[:], a[:, lo:hi], ACT.Identity, scale=gamma[:])
+            nc.vector.tensor_tensor(
+                placed[:].indirect(offsets[:, lo // 16 : hi // 16]), term_w[:, lo:hi], term_a[:], ALU.add
+            )
 
         start = 0
         for n, width in enumerate(STORE_WIDTHS):

@@ -17,10 +17,12 @@ ACT = mybir.ActivationFunctionType
 
 P = 128
 PACK = 4
-VALS_ROW0 = 4
+STRIPE = 16
+GS_FACTOR = 2.0 * 512.0
+KEY_ROW0, VAL_ROW0 = 0, 4
 HALF = I // 2
-KEY_SPLIT = 3 * T // 4
-STORE_WIDTHS = (256, 512, 512, 512, 256)
+KEY_SPLIT = T // 2
+STORE_WIDTHS = (128, 384, 512, 512, 384, 128)
 
 
 def tile_attend_hvsquareshares_s_kernel(
@@ -31,17 +33,14 @@ def tile_attend_hvsquareshares_s_kernel(
         keep = ctx.enter_context(tc.tile_pool(name="keep", bufs=1))
         psum = ctx.enter_context(tc.psum_pool(name="psum", bufs=1))
 
-        def sb(name, width, dtype, tag=None):
-            return keep.tile([P, width], dtype, name=name, tag=tag or name, align_bytes=64)
+        def sb(name, width, dtype, reuses=None):
+            return keep.tile([P, width], dtype, name=name, tag=reuses or name, align_bytes=64)
 
-        offsets = keep.tile([P, I // 16], U16, name="offsets")
-        nc.sync.dma_start(offsets[:], offs)
-
-        def load_scales(name, scales, row0, queues):
+        def load_scales(name, scales, row0):
             plane = sb(name, T, U8)
             nc.vector.memset(plane[:].bitcast(I32), 0)
             for quad in range(4):
-                queues[quad].dma_start(
+                nc.sync.dma_start(
                     plane[32 * quad + row0 : 32 * quad + row0 + 4, :].bitcast(I32),
                     scales[0, 4 * quad : 4 * quad + 4, :].bitcast(I32),
                 )
@@ -50,51 +49,57 @@ def tile_attend_hvsquareshares_s_kernel(
         def load_words(pool, words, cols):
             nc.sync.dma_start(pool[:, cols], words[0].rearrange("p n t -> p (n t)").bitcast(I32)[:, cols])
 
-        def load_rows(name, rows, tag):
-            raw = keep.tile([P, PACK, Q], F32, name=name, tag=tag, align_bytes=64)
+        def load_rows(name, rows):
+            raw = keep.tile([P, PACK, Q], F32, name=name, tag=name, align_bytes=64)
             nc.sync.dma_start(raw[:], rows.rearrange("(p j) q -> p j q", j=PACK))
             return raw
 
-        def gather(name, pool, dtype, tag=None):
-            picked = sb(name, I, dtype, tag)
-            nc.vector.tensor_copy(picked[:], pool.indirect(offsets[:]))
+        def gather_scales(name, pool):
+            picked = sb(name, I, U8)
+            nc.vector.tensor_copy(picked[:], pool[:].indirect(offsets[:]))
             return picked
 
-        def quantise(name, raw, tag=None):
+        def quantise(name, raw):
             woven = keep.tile([P, Q, PACK], BF16, name=name + "_woven", align_bytes=64)
             nc.scalar.copy(woven[:], raw[:].rearrange("p j q -> p q j"))
-            codes = sb(name + "_codes", Q, U32, tag)
+            codes = sb(name + "_codes", Q, U32)
             plane = sb(name + "_plane", Q, U8)
             nc.vector.quantize_mx(
                 out=codes[:].bitcast(FP8X4), scales=plane[:], in_=woven[:].rearrange("p q j -> p (q j)")
             )
             return codes, plane
 
-        def gather_and_score(name, pool, plane, row0, products, tag=None):
-            picked = sb(name, I, U32, tag)
+        def gather_and_score(name, pool, picked_plane, row0, products):
+            picked = sb(name, I, U32)
             for lo in range(0, I, HALF):
                 cols = slice(lo, lo + HALF)
-                listed = offsets[:, lo // 16 : (lo + HALF) // 16]
+                listed = offsets[:, lo // STRIPE : (lo + HALF) // STRIPE]
                 nc.vector.tensor_copy(picked[:, cols], pool[:].bitcast(U32).indirect(listed))
-                for bank, (codes, code_plane) in products:
+                for halves, (codes, plane) in products:
                     nc.tensor.matmul_mx(
-                        out=bank[:, cols], lhsT=codes[:].bitcast(FP8X4), lhsT_scale=code_plane[:],
-                        rhs=picked[:, cols].bitcast(FP8X4), rhs_scale=plane[row0:P, cols], start=True, stop=True,
+                        out=halves[lo // HALF],
+                        lhsT=codes[:].bitcast(FP8X4),
+                        lhsT_scale=plane[:],
+                        rhs=picked[:, cols].bitcast(FP8X4),
+                        rhs_scale=picked_plane[row0:P, cols],
+                        start=True,
+                        stop=True,
                     )
 
+        offsets = keep.tile([P, I // STRIPE], U16, name="offsets")
+        nc.sync.dma_start(offsets[:], offs)
         floor_sb = sb("floor_sb", 1, F32)
         reserve_sb = sb("reserve_sb", 1, F32)
-        nc.scalar.dma_start(floor_sb[:], floor)
-        nc.scalar.dma_start(reserve_sb[:], reserve)
-
+        nc.gpsimd.dma_start(floor_sb[:], floor)
+        nc.gpsimd.dma_start(reserve_sb[:], reserve)
         key_pool = sb("key_pool", T, I32)
         load_words(key_pool, keys_words, slice(0, KEY_SPLIT))
-        key_scale_pool = load_scales("key_scale_pool", keys_scales, 0, [nc.sync] * 4)
-        query_raw = load_rows("query_raw", query, "query_raw")
-        dquery_raw = load_rows("dquery_raw", dquery, "dquery_raw")
+        key_scale_pool = load_scales("key_scale_pool", keys_scales, KEY_ROW0)
+        query_raw = load_rows("query_raw", query)
+        dquery_raw = load_rows("dquery_raw", dquery)
         load_words(key_pool, keys_words, slice(KEY_SPLIT, T))
-        gout_raw = load_rows("gout_raw", gout, "gout_raw")
-        val_scale_pool = load_scales("val_scale_pool", vals_scales, VALS_ROW0, [nc.sync] * 4)
+        gout_raw = load_rows("gout_raw", gout)
+        val_scale_pool = load_scales("val_scale_pool", vals_scales, VAL_ROW0)
         val_pool = sb("val_pool", T, I32)
         load_words(val_pool, vals_words, slice(0, T))
         base_sb = sb("base_sb", T, F32)
@@ -102,72 +107,68 @@ def tile_attend_hvsquareshares_s_kernel(
         placed = sb("placed", T, F32)
         nc.vector.memset(placed[:], 0.0)
 
-        key_plane = gather("key_plane", key_scale_pool[:], U8)
+        key_plane = gather_scales("key_plane", key_scale_pool)
         query_mx = quantise("query", query_raw)
         dquery_mx = quantise("dquery", dquery_raw)
-        a = psum.tile([P, I], F32, name="a")
+        a_banks = [psum.tile([P, HALF], F32, name=f"a{h}") for h in range(2)]
         ta = psum.tile([P, I], F32, name="ta")
-        gather_and_score("keys", key_pool, key_plane, 0, ((a, query_mx), (ta, dquery_mx)))
+        a_halves = [bank[:] for bank in a_banks]
+        ta_halves = [ta[:, 0:HALF], ta[:, HALF:I]]
+        gather_and_score("keys", key_pool, key_plane, KEY_ROW0, ((a_halves, query_mx), (ta_halves, dquery_mx)))
         gout_mx = quantise("gout", gout_raw)
-        val_plane = gather("val_plane", val_scale_pool[:], U8)
+        val_plane = gather_scales("val_plane", val_scale_pool)
 
-        floor_k = sb("floor_k", 1, F32)
-        nc.scalar.activation(floor_k[:], floor_sb[:], ACT.Identity, scale=1.0 / 1024)
-        reserve_k = sb("reserve_k", 1, F32)
-        nc.scalar.activation(reserve_k[:], reserve_sb[:], ACT.Identity, scale=-1.0 / 1024)
-        fixed = sb("fixed", 1, F32)
-        nc.scalar.activation(fixed[:], floor_sb[:], ACT.Identity, scale=-float(I) / 1024, bias=reserve_k[:])
-
-        a_sb = sb("a_sb", I, F32, "gout_raw")
-        nc.scalar.copy(a_sb[:], a[:])
+        neg_fixed = sb("neg_fixed", 1, F32)
+        nc.gpsimd.tensor_scalar(neg_fixed[:], floor_sb[:], -float(I), reserve_sb[:], ALU.mult, ALU.subtract)
+        a = sb("a", I, F32, reuses="gout_raw")
+        for h in range(2):
+            nc.scalar.copy(a[:, h * HALF : (h + 1) * HALF], a_halves[h])
         sq = sb("sq", I, F32)
         sq_sum = sb("sq_sum", 1, F32)
-        nc.scalar.activation(sq[:], a[:], ACT.Square, scale=1.0 / 32, accum_out=sq_sum[:])
+        nc.scalar.activation(sq[:], a[:], ACT.Square, accum_out=sq_sum[:])
         neg_z = sb("neg_z", 1, F32)
-        nc.scalar.activation(neg_z[:], sq_sum[:], ACT.Identity, scale=-1.0, bias=fixed[:])
+        nc.scalar.activation(neg_z[:], sq_sum[:], ACT.Identity, scale=-1.0, bias=neg_fixed[:])
 
-        at_and_alpha = sb("at_and_alpha", I + 1, F32, "val_scale_pool")
-        at = at_and_alpha[:, 0:I]
-        neg_alpha = at_and_alpha[:, I : I + 1]
-        at_sum = sb("at_sum", 1, F32)
-        nc.vector.scalar_tensor_tensor(at, ta[:], -1.0 / 512, a_sb[:], ALU.mult, ALU.mult, accum_out=at_sum[:])
-        nc.vector.reciprocal(neg_alpha, neg_z[:])
-        alpha2 = sb("alpha2", 1, F32)
-        nc.scalar.activation(alpha2[:], neg_alpha, ACT.Square)
-        beta = sb("beta", 1, F32)
-        nc.scalar.activation(beta[:], at_sum[:], ACT.Identity, scale=alpha2[:])
-        neg_x = sb("neg_x", I, F32)
-        nc.scalar.activation(neg_x[:], ta[:], ACT.Identity, scale=neg_alpha)
+        tp_and_r = sb("tp_and_r", I + 1, F32, reuses="val_scale_pool")
+        tp = tp_and_r[:, 0:I]
+        neg_r = tp_and_r[:, I : I + 1]
+        tz = sb("tz", 1, F32)
+        nc.vector.scalar_tensor_tensor(tp, ta[:], 2.0, a[:], ALU.mult, ALU.mult, accum_out=tz[:])
+        nc.vector.reciprocal(neg_r, neg_z[:])
+        rho = sb("rho", 1, F32)
+        nc.scalar.activation(rho[:], tz[:], ACT.Identity, scale=neg_r)
+        row_scale = sb("row_scale", 1, F32)
+        nc.scalar.activation(row_scale[:], neg_r, ACT.Identity, scale=-GS_FACTOR)
 
         c0 = psum.tile([P, I], F32, name="c0")
-        gather_and_score("vals", val_pool, val_plane, VALS_ROW0, ((c0, gout_mx),), "gout_raw")
+        gather_and_score("vals", val_pool, val_plane, VAL_ROW0, (([c0[:, 0:HALF], c0[:, HALF:I]], gout_mx),))
 
-        w = sb("w", I, F32, "val_pool")
-        nc.vector.scalar_tensor_tensor(w[:], a[:], beta[:], neg_x[:], ALU.mult, ALU.subtract)
+        w = sb("w", I, F32, reuses="val_pool")
+        nc.vector.scalar_tensor_tensor(w[:], a[:], rho[:], ta[:], ALU.mult, ALU.add)
 
         cp = sb("cp", I, F32)
         cp_sum = sb("cp_sum", 1, F32)
-        nc.vector.scalar_tensor_tensor(cp[:], sq[:], floor_k[:], c0[:], ALU.add, ALU.mult, accum_out=cp_sum[:])
-        cat = sb("cat", I, F32)
-        cat_sum = sb("cat_sum", 1, F32)
-        nc.vector.scalar_tensor_tensor(cat[:], at, alpha2[:], c0[:], ALU.mult, ALU.mult, accum_out=cat_sum[:])
+        nc.vector.scalar_tensor_tensor(cp[:], sq[:], floor_sb[:], c0[:], ALU.add, ALU.mult, accum_out=cp_sum[:])
+        ctp = sb("ctp", I, F32)
+        ctp_sum = sb("ctp_sum", 1, F32)
+        nc.vector.scalar_tensor_tensor(ctp[:], tp, neg_r, c0[:], ALU.mult, ALU.mult, accum_out=ctp_sum[:])
         eps = sb("eps", 1, F32)
-        nc.scalar.activation(eps[:], cp_sum[:], ACT.Identity, scale=neg_alpha)
+        nc.scalar.activation(eps[:], cp_sum[:], ACT.Identity, scale=neg_r)
         gamma = sb("gamma", 1, F32)
-        nc.scalar.activation(gamma[:], eps[:], ACT.Identity, scale=beta[:], bias=cat_sum[:])
+        nc.scalar.activation(gamma[:], eps[:], ACT.Identity, scale=rho[:], bias=ctp_sum[:])
+
         term_w = sb("term_w", I, F32)
         nc.vector.scalar_tensor_tensor(term_w[:], c0[:], eps[:], w[:], ALU.add, ALU.mult)
-        for n, (lo, hi) in enumerate(((0, I),)):
-            term_a = sb(f"term_a{n}", hi - lo, F32)
-            nc.scalar.activation(term_a[:], a[:, lo:hi], ACT.Identity, scale=gamma[:])
-            nc.vector.tensor_tensor(
-                placed[:].indirect(offsets[:, lo // 16 : hi // 16]), term_w[:, lo:hi], term_a[:], ALU.add
-            )
+        term_a = sb("term_a", I, F32)
+        nc.scalar.activation(term_a[:], a[:], ACT.Identity, scale=gamma[:])
+        nc.vector.tensor_tensor(placed[:].indirect(offsets[:]), term_w[:], term_a[:], ALU.add)
 
         start = 0
         for n, width in enumerate(STORE_WIDTHS):
             cols = slice(start, start + width)
             piece = sb(f"piece{n}", width, F32)
-            nc.vector.tensor_tensor(piece[:], placed[:, cols], base_sb[:, cols], ALU.add)
+            nc.vector.scalar_tensor_tensor(
+                piece[:], placed[:, cols], row_scale[:], base_sb[:, cols], ALU.mult, ALU.add
+            )
             nc.sync.dma_start(out[:, cols], piece[:])
             start = start + width

from contextlib import ExitStack

import concourse.mybir as mybir

D, T, I, Q = 512, 2048, 512, 128
FLOPS = 3 * 2 * D * Q * I

F32 = mybir.dt.float32
BF16 = mybir.dt.bfloat16
I32 = mybir.dt.int32
U32 = mybir.dt.uint32
U16 = mybir.dt.uint16
U8 = mybir.dt.uint8
FP8X4 = mybir.dt.float8_e4m3fn_x4
ALU = mybir.AluOpType
ACT = mybir.ActivationFunctionType

P = 128
PACK = 4
STRIPE = 16
GS_FACTOR = 2.0 * 512.0
KEY_ROW0, VAL_ROW0 = 0, 4
HALF = I // 2
KEY_SPLIT = T // 2
STORE_WIDTHS = (128, 384, 512, 512, 384, 128)


def tile_attend_hvsquareshares_s_kernel(
    tc, query, keys_words, keys_scales, floor, reserve, gout, vals_words, vals_scales, dquery, base, offs, out
):
    nc = tc.nc
    with ExitStack() as ctx:
        keep = ctx.enter_context(tc.tile_pool(name="keep", bufs=1))
        psum = ctx.enter_context(tc.psum_pool(name="psum", bufs=1))

        def sb(name, width, dtype, reuses=None):
            return keep.tile([P, width], dtype, name=name, tag=reuses or name, align_bytes=64)

        def load_scales(name, scales, row0):
            plane = sb(name, T, U8)
            nc.vector.memset(plane[:].bitcast(I32), 0)
            for quad in range(4):
                nc.sync.dma_start(
                    plane[32 * quad + row0 : 32 * quad + row0 + 4, :].bitcast(I32),
                    scales[0, 4 * quad : 4 * quad + 4, :].bitcast(I32),
                )
            return plane

        def load_words(pool, words, cols):
            nc.sync.dma_start(pool[:, cols], words[0].rearrange("p n t -> p (n t)").bitcast(I32)[:, cols])

        def load_rows(name, rows):
            raw = keep.tile([P, PACK, Q], F32, name=name, tag=name, align_bytes=64)
            nc.sync.dma_start(raw[:], rows.rearrange("(p j) q -> p j q", j=PACK))
            return raw

        def gather_scales(name, pool):
            picked = sb(name, I, U8)
            nc.vector.tensor_copy(picked[:], pool[:].indirect(offsets[:]))
            return picked

        def quantise(name, raw):
            woven = keep.tile([P, Q, PACK], BF16, name=name + "_woven", align_bytes=64)
            nc.scalar.copy(woven[:], raw[:].rearrange("p j q -> p q j"))
            codes = sb(name + "_codes", Q, U32)
            plane = sb(name + "_plane", Q, U8)
            nc.vector.quantize_mx(
                out=codes[:].bitcast(FP8X4), scales=plane[:], in_=woven[:].rearrange("p q j -> p (q j)")
            )
            return codes, plane

        def gather_and_score(name, pool, picked_plane, row0, products):
            picked = sb(name, I, U32)
            for lo in range(0, I, HALF):
                cols = slice(lo, lo + HALF)
                listed = offsets[:, lo // STRIPE : (lo + HALF) // STRIPE]
                nc.vector.tensor_copy(picked[:, cols], pool[:].bitcast(U32).indirect(listed))
                for halves, (codes, plane) in products:
                    nc.tensor.matmul_mx(
                        out=halves[lo // HALF],
                        lhsT=codes[:].bitcast(FP8X4),
                        lhsT_scale=plane[:],
                        rhs=picked[:, cols].bitcast(FP8X4),
                        rhs_scale=picked_plane[row0:P, cols],
                        start=True,
                        stop=True,
                    )

        offsets = keep.tile([P, I // STRIPE], U16, name="offsets")
        nc.sync.dma_start(offsets[:], offs)
        floor_sb = sb("floor_sb", 1, F32)
        reserve_sb = sb("reserve_sb", 1, F32)
        nc.gpsimd.dma_start(floor_sb[:], floor)
        nc.gpsimd.dma_start(reserve_sb[:], reserve)
        key_pool = sb("key_pool", T, I32)
        load_words(key_pool, keys_words, slice(0, KEY_SPLIT))
        key_scale_pool = load_scales("key_scale_pool", keys_scales, KEY_ROW0)
        query_raw = load_rows("query_raw", query)
        dquery_raw = load_rows("dquery_raw", dquery)
        load_words(key_pool, keys_words, slice(KEY_SPLIT, T))
        gout_raw = load_rows("gout_raw", gout)
        val_scale_pool = load_scales("val_scale_pool", vals_scales, VAL_ROW0)
        val_pool = sb("val_pool", T, I32)
        load_words(val_pool, vals_words, slice(0, T))
        base_sb = sb("base_sb", T, F32)
        nc.sync.dma_start(base_sb[:], base)
        placed = sb("placed", T, F32)
        nc.vector.memset(placed[:], 0.0)

        key_plane = gather_scales("key_plane", key_scale_pool)
        query_mx = quantise("query", query_raw)
        dquery_mx = quantise("dquery", dquery_raw)
        a_banks = [psum.tile([P, HALF], F32, name=f"a{h}") for h in range(2)]
        ta = psum.tile([P, I], F32, name="ta")
        a_halves = [bank[:] for bank in a_banks]
        ta_halves = [ta[:, 0:HALF], ta[:, HALF:I]]
        gather_and_score("keys", key_pool, key_plane, KEY_ROW0, ((a_halves, query_mx), (ta_halves, dquery_mx)))
        gout_mx = quantise("gout", gout_raw)
        val_plane = gather_scales("val_plane", val_scale_pool)

        neg_fixed = sb("neg_fixed", 1, F32)
        nc.gpsimd.tensor_scalar(neg_fixed[:], floor_sb[:], -float(I), reserve_sb[:], ALU.mult, ALU.subtract)
        a = sb("a", I, F32, reuses="gout_raw")
        for h in range(2):
            nc.scalar.copy(a[:, h * HALF : (h + 1) * HALF], a_halves[h])
        sq = sb("sq", I, F32)
        sq_sum = sb("sq_sum", 1, F32)
        nc.scalar.activation(sq[:], a[:], ACT.Square, accum_out=sq_sum[:])
        neg_z = sb("neg_z", 1, F32)
        nc.scalar.activation(neg_z[:], sq_sum[:], ACT.Identity, scale=-1.0, bias=neg_fixed[:])

        tp_and_r = sb("tp_and_r", I + 1, F32, reuses="val_scale_pool")
        tp = tp_and_r[:, 0:I]
        neg_r = tp_and_r[:, I : I + 1]
        tz = sb("tz", 1, F32)
        nc.vector.scalar_tensor_tensor(tp, ta[:], 2.0, a[:], ALU.mult, ALU.mult, accum_out=tz[:])
        nc.vector.reciprocal(neg_r, neg_z[:])
        rho = sb("rho", 1, F32)
        nc.scalar.activation(rho[:], tz[:], ACT.Identity, scale=neg_r)
        row_scale = sb("row_scale", 1, F32)
        nc.scalar.activation(row_scale[:], neg_r, ACT.Identity, scale=-GS_FACTOR)

        c0 = psum.tile([P, I], F32, name="c0")
        gather_and_score("vals", val_pool, val_plane, VAL_ROW0, (([c0[:, 0:HALF], c0[:, HALF:I]], gout_mx),))

        w = sb("w", I, F32, reuses="val_pool")
        nc.vector.scalar_tensor_tensor(w[:], a[:], rho[:], ta[:], ALU.mult, ALU.add)

        cp = sb("cp", I, F32)
        cp_sum = sb("cp_sum", 1, F32)
        nc.vector.scalar_tensor_tensor(cp[:], sq[:], floor_sb[:], c0[:], ALU.add, ALU.mult, accum_out=cp_sum[:])
        ctp = sb("ctp", I, F32)
        ctp_sum = sb("ctp_sum", 1, F32)
        nc.vector.scalar_tensor_tensor(ctp[:], tp, neg_r, c0[:], ALU.mult, ALU.mult, accum_out=ctp_sum[:])
        eps = sb("eps", 1, F32)
        nc.scalar.activation(eps[:], cp_sum[:], ACT.Identity, scale=neg_r)
        gamma = sb("gamma", 1, F32)
        nc.scalar.activation(gamma[:], eps[:], ACT.Identity, scale=rho[:], bias=ctp_sum[:])

        term_w = sb("term_w", I, F32)
        nc.vector.scalar_tensor_tensor(term_w[:], c0[:], eps[:], w[:], ALU.add, ALU.mult)
        term_a = sb("term_a", I, F32)
        nc.scalar.activation(term_a[:], a[:], ACT.Identity, scale=gamma[:])
        nc.vector.tensor_tensor(placed[:].indirect(offsets[:]), term_w[:], term_a[:], ALU.add)

        start = 0
        for n, width in enumerate(STORE_WIDTHS):
            cols = slice(start, start + width)
            piece = sb(f"piece{n}", width, F32)
            nc.vector.scalar_tensor_tensor(
                piece[:], placed[:, cols], row_scale[:], base_sb[:, cols], ALU.mult, ALU.add
            )
            nc.sync.dma_start(out[:, cols], piece[:])
            start = start + width
